import numpy as np, ml_dtypes
CORES = [2,3,42,43,82,83,122,123]
N = 8
BF = ml_dtypes.bfloat16
V, K, LA, LF, Q, RO, AS, FS = 3072, 1536, 256, 192, 5, 3, 256, 512
def lanes(flag, start, cap):
    order = (np.arange(K) + start) % K; fl = flag[:, order]
    o = np.argsort(~fl, axis=1, kind="stable")[:, :cap]
    return order[o], np.take_along_axis(fl, o, 1)
def judge(X, C, ids, T):
    n = ids.shape[1]; lit = np.take_along_axis(C, ids[:, None, :], 2); v = np.where(lit >= V, lit - V, lit)
    s = np.take_along_axis(X, v.reshape(8, 1, 16 * n), 2).reshape(8, 16, 16, n)
    s = np.where((lit >= V)[:, None], 63 - s, s)
    return lit, v, s, np.max(s, axis=2) < T
def states(rng, pa, pd):
    a = rng.choice(np.array(pa), (N, 8, 1)); b = rng.choice(np.array(pd), (N, 8, 1)); u = rng.random((N, 8, K))
    return np.where(u < a, 0, np.where(u >= 1 - b, 4, rng.integers(1, 4, (N, 8, K))))
def parts(rng):
    u = rng.random((N, 8, 16, K)); v = np.minimum((V * u * np.sqrt(u)).astype(np.int64), V - 1)
    T = rng.integers(58, 60, (N, 8, 1, 1)) + rng.integers(0, 2, (N, 8, 16, 1))
    return rng.integers(0, 64, (N, 8, 16, V)), v + V * rng.integers(0, 2, v.shape), states(rng, [0.3, 0.4, 0.5], [0.01, 0.05, 0.2]), T
def at(a, v):
    return np.take_along_axis(a, v.reshape(N, 8, -1), 2).reshape(v.shape)
def first(X, C, F, T):
    ia, ok = lanes(F == 0, 0, LA)
    return ia, ok & (np.sum(judge(X, C, ia, T)[3], axis=1) > Q)
def laid(rng, own, place, rest):
    X = np.zeros((8, 16, V), np.int64); C = np.zeros((8, 16, K), np.int64)
    for g in range(8):
        o = rng.permutation(V); sign = rng.integers(0, 2, V)
        s = rng.integers(0, rest[g] + 1, (16, V)); s[:, o[:K]] = own[g]
        X[g] = np.where(sign == 1, 63 - s, s)
        v = o[rng.integers(K, V, (16, K))]; v[place[g], np.arange(K)] = o[:K]
        C[g] = v + V * sign[v]
    return X, C
def full(rng):
    T = rng.integers(50, 61, (8, 16, 1)); own = rng.integers(10, 18, (8, 16, K)); place = rng.integers(0, 16, (8, K)); F = np.zeros((8, K), np.int64)
    own[[2, 7]] = 0; place[[2, 7]] = 0
    for g in range(8):
        o = rng.permutation(K); n = int(rng.integers(16, LF + 1))
        F[g, o[:n]] = rng.integers(1, 4, n); F[g, o[:16]] = 1
        own[g][:, o[:16]] = T[g] + rng.integers(0, 3, (16, 16))
    X, C = laid(rng, own, place, [9, 9, 0, 9, 9, 9, 9, 0])
    return X, C, F, T
def calm(rng):
    T = rng.integers(20, 51, (8, 16, 1)); own = np.repeat(T, K, axis=2); place = rng.integers(0, 16, (8, K)); F = rng.integers(1, 3, (8, K)); e = int(rng.integers(1, 4))
    for g in range(8):
        o = rng.permutation(K); n = 4 * int(rng.integers(2, LA >> 4)) + (e if g == 0 else 0); m = n + int(rng.integers(0, LA - n + 1)); h = m + ((K - m) >> 1)
        F[g, o[:m]] = 0
        own[g][:, o[n:h]] = 63; own[g][:, o[:n]] = T[g] - rng.integers(1, 6, (16, n))
    X, C = laid(rng, own, place, [9] * 8)
    return X, C, F, T
def pack(X, C, F, T):
    return {"xv": np.ascontiguousarray(X).reshape(N, 128, V).astype(np.float32).astype(BF), "cl": np.ascontiguousarray(C).reshape(N, 128, K).astype(np.int32),
            "fr": np.ascontiguousarray(F).astype(np.int32), "th": np.ascontiguousarray(T).reshape(N, 128, 1).astype(np.int32)}
def setup_inputs(rng):
    X, C, F, T = parts(rng)
    return pack(X, C, F, T)
def setup_inputs_spread(rng):
    low = np.minimum(np.exp2(6 * rng.random((N, 8, 1, V))) * rng.random((N, 8, 16, V)), 63).astype(np.int64)
    flip = rng.random((N, 8, V)) < 0.5; X = np.where(flip[:, :, None], 63 - low, low)
    u = rng.random((N, 8, 16, K)); v = np.minimum((V * u * u).astype(np.int64), V - 1)
    up = rng.random(v.shape) < rng.choice(np.array([0.0, 0.02, 0.06, 0.12]), (N, 8, 1, K))
    T = np.clip(61 - np.exp2(5.907 * rng.random((N, 8, 16, 1))).astype(np.int64), 1, 60)
    return pack(X, v + V * (at(flip, v) ^ up).astype(np.int64), states(rng, [0.1, 0.3, 0.6, 0.9], [0.0, 0.02, 0.3]), T)
def setup_inputs_ends(rng):
    X = 63 * rng.integers(0, 2, (N, 8, 16, V)); k = np.arange(16)[:, None]
    T = np.where(rng.random((N, 8, 16, 1)) < 0.75, 60, 1); T[:, [3, 7]] = 60; T[:, 0, 0] = 1
    u = rng.random((N, 8, K)); F = np.where(u < 0.45, 0, np.where(u < 0.75, 4, rng.choice(np.array([1, 3]), (N, 8, K))))
    m = rng.choice(np.array([16, 16, Q + 1, Q]), (N, 8, 1)); m[:, 1] = Q + 1; m[:, 2] = Q; m[:, [3, 7]] = 16
    low = np.argsort(np.argsort(rng.random((N, 8, 16)), axis=2), axis=2) < m
    X[..., 0] = np.where(low, 0, 63); X[..., V - 1] = np.where(low, 63, 0); X[..., 65] = 63
    sp = np.concatenate([np.arange(1, 65), np.arange(V - 65, V - 1)]); j = np.arange(128); cls = (j >> 1) % 3
    s = np.where(cls == 0, 59, np.where((cls == 2) & (k > Q), 63, 62)) - ((j // 6) % 2) * (k == j % 16)
    X[..., sp] = np.where(j % 2 == 1, 63 - s, s); lit = sp + V * (j % 2)
    C = np.where(rng.random((N, 8, 16, K)) < rng.choice(np.array([0.0, 0.5, 0.5, 1.0]), (N, 8, 1, K)), 0, 2 * V - 1)
    kind = rng.choice(np.array([0, 0, 0, 0, 0, 0, 0, 1, 2, 3]), (N, 8, K)); frm = rng.integers(0, 16, (N, 8, K))
    for q in range(N):
        F[q, 7] = 4; kind[q, 7] = rng.choice(np.array([0, 0, 1]), K)
        b = np.append(np.sort(AS + rng.permutation(K - 1 - AS)[:LA - 1]), K - 1)
        F[q, 7, rng.permutation(AS)[:32]] = 0; F[q, 7, b] = 0
        kind[q, 7, b[-32:]] = 2; kind[q, 7, b[-2:]] = 3; frm[q, 7, b[-2:]] = 0
    for c in range(3):
        a = lit[cls == c]; fill = a[rng.integers(0, len(a), C.shape)]
        C = np.where((kind == c + 1)[:, :, None] & (k >= frm[:, :, None]), fill, C)
    for q in range(N):
        ia, bad = first(X[q], C[q], F[q], T[q]); b = np.flatnonzero(bad[3])[:(int(np.sum(bad)) - 3) % 4]
        C[q, 3, 8, ia[3, b]] = 65
    return pack(X, C, F, T)
def setup_inputs_corners(rng):
    X, C, F, T = parts(rng); w = rng.random((N, 8, 1, K)); e = np.array([0, V - 1, V, 2 * V - 1])
    C = np.where(w < 0.15, rng.choice(e, (N, 8, 1, K)), np.where(w < 0.3, np.arange(K) + V * rng.integers(0, 2, (N, 8, 1, K)), np.where(w < 0.45, rng.choice(e, (N, 8, 16, K)), C)))
    T[:, 1] = np.where(rng.random((N, 16, 1)) < 0.3, 1, 60); T[:, 5] = 1; T[:, 6] = 60
    cases = ((0, K), (K, 0), (LA, LF), (LA + 1, LF + 1), (LA - 1, LF - 1), (1, 0), (2, K - 2), (0, 0))
    for q in range(N):
        for g in range(8):
            na, nz = cases[(g + q) % 8]; o = rng.permutation(K)
            F[q, g] = 4; F[q, g, o[:na]] = 0; F[q, g, o[na:na + nz]] = rng.integers(1, 4, nz)
    for q in range(0, N - 1, 2):
        bad = first(X[q], C[q], F[q], T[q])[1]; n = np.sum(bad[:, 0::2] & bad[:, 1::2], axis=1); c = 0
        for g in range(8):
            if n[g] < 2: continue
            d = int(n[g]) + (0, 1, -1)[c % 3]; c += 1
            z = rng.integers(0, 4, K); z[rng.permutation(K)[:d]] = 4; F[q + 1, g] = z
    return pack(X, C, F, T)
def setup_inputs_ties(rng):
    b = rng.choice(np.array([9, 30, 60]), (N, 8, 1, 1)); T = np.zeros((N, 8, 16, 1), np.int64) + b; i = np.arange(16)[:, None]
    mul = 2 * rng.integers(0, 8, (N, 8, 1, V)) + 1; sh = rng.integers(0, 16, (N, 8, 1, V)); n = Q + rng.integers(0, 2, (N, 8, 1, V))
    odd = np.arange(V) % 2 == 1
    s = np.where(odd & ((i * mul + sh) % 16 >= n), b + rng.integers(0, 4, (N, 8, 1, V)), b - 1 - rng.integers(0, 2, (N, 8, 1, V)))
    flip = rng.random((N, 8, V)) < 0.5; X = np.where(flip[:, :, None], 63 - s, s)
    lim = rng.choice(np.array([V // 2, V // 2, V // 16]), (N, 8, 1, 1))
    v = 2 * np.minimum((rng.random((N, 8, 16, K)) * lim).astype(np.int64), lim - 1)
    one = (i == rng.integers(0, 16, (N, 8, 1, K))) & (rng.random((N, 8, 1, K)) < 0.9)
    v = np.where(one, 2 * rng.integers(0, V // 2, v.shape) + 1, v)
    return pack(X, v + V * at(flip, v).astype(np.int64), states(rng, [0.3, 0.4, 0.5], [0.02, 0.1, 0.2]), T)
def setup_inputs_alike(rng):
    X, C, F, T = parts(rng); few = rng.integers(0, V, (N, 8, 24)); few[:, :, 0] = 0; few[:, :, 1] = V - 1
    v = np.take_along_axis(few, rng.integers(0, 24, (N, 8, 16 * K)), 2).reshape(N, 8, 16, K) + V * rng.integers(0, 2, (N, 8, 16, K))
    C[:, ::2] = v[:, ::2]
    for q in range(N): C[q, 5] = C[q, 5][:, rng.integers(0, 8, K)]
    o = rng.permutation(N)
    X[o[0]], C[o[0]], F[o[0]], T[o[0]] = full(rng)
    X[o[1]], C[o[1]], F[o[1]], T[o[1]] = calm(rng)
    return pack(X, C, F, T)
def check_inputs(d):
    bad = []
    for k, lo, hi in (("xv", 0, 63), ("cl", 0, 2 * V - 1), ("fr", 0, 4), ("th", 1, 60)):
        a = np.asarray(d[k]).astype(np.float64)
        if not np.all((a >= lo) & (a <= hi)): bad.append("range of " + k)
        elif not np.all(a == np.floor(a)): bad.append("whole numbers of " + k)
    return bad
def reference(xv, cl, fr, th):
    X = xv.astype(np.float32).astype(np.int64).reshape(N, 8, 16, V); C = cl.astype(np.int64).reshape(N, 8, 16, K); F = fr.astype(np.int64).reshape(N, 8, K)
    TH = th.astype(np.int64).reshape(N, 8, 16, 1); A = np.zeros(N, np.int64)
    for t in range(RO):
        nX = np.array(X); nC = np.array(C); nF = np.array(F); sent = []
        for r in range(N):
            T = TH[r] + (A[r] & 3)
            ia, oka = lanes(F[r] == 0, AS * t % K, LA); iz, okz = lanes((F[r] >= 1) & (F[r] <= 3), FS * t % K, LF)
            lit, v, s, fail = judge(X[r], C[r], ia, T); bad = oka & (np.sum(fail, axis=1) > Q); A[r] = np.sum(bad)
            m = oka & ~bad; nF[r][np.nonzero(m)[0], ia[m]] = 1
            wake = np.sum(judge(X[r], C[r], iz, T)[3], axis=1) > Q
            old = np.take_along_axis(F[r], iz, 1); nF[r][np.nonzero(okz)[0], iz[okz]] = np.where(wake, 0, old + 1)[okz]
            kk = np.argmax(np.sum(s * fail[:, :, None, :], axis=1), axis=1)[:, None, :]
            pick = np.take_along_axis(lit, kk, 1); pv = np.take_along_axis(v, kk, 1)[:, 0]
            up = np.minimum(np.take_along_axis(s, kk[:, None], 2)[:, :, 0] + 8, 63); new = np.where(pick >= V, 63 - up, up)
            for g in range(8):
                b = np.flatnonzero(bad[g]); u, ix = np.unique(pv[g, b], return_index=True); w = b[ix]
                nX[r, g][:, u] = np.where(fail[g][:, w], new[g][:, w], X[r, g][:, u])
            tot = np.sum(s, axis=1)
            sent.append((bad[:, 0::2] & bad[:, 1::2], np.where(tot[:, :, 1::2] > tot[:, :, 0::2], lit[:, :, 1::2], lit[:, :, 0::2])))
        for r in range(N):
            a = (r + 1 + t % 3) % N; both, joint = sent[r]
            for g in range(8):
                come = joint[g][:, both[g]]; dead = np.flatnonzero(F[a, g] == 4); n = min(come.shape[1], len(dead))
                nC[a, g][:, dead[:n]] = come[:, :n]; nF[a, g][dead[:n]] = 0
        X = nX; C = nC; F = nF
    return {"yx": X.reshape(N, 128, V).astype(np.float32).astype(BF), "yc": C.reshape(N, 128, K).astype(np.float32), "yf": F.astype(np.float32)}

@@ -1,0 +1,445 @@
+from concourse.mybir import AluOpType as O, ActivationFunctionType as AF
+
+BA, BZ, BD, BR, RW = 0, 1536, 3072, 4608, 132
+BIG = 8191.0
+A1, A2 = 80, 176
+PARTS = ((0, 128), (128, 192), (192, 256))
+f, b, i32, u16 = "float32", "bfloat16", "int32", "uint16"
+BUFS = {
+    "S": (6656, b), "s": (4096, b), "ind": (4096, b), "indz": (3072, b), "pr": (4096, b), "W": (BR + 3 * RW, f),
+    "CLI": (1536, i32), "CLF": (1536, f), "VD": (4608, b), "DR": (1536, b), "E": (4096, b), "F": (96, b),
+    "FL": (288, b), "g1": (96, b), "IL": (288, f), "rz": (288, f), "m1": (96, f), "code": (96, f), "cU": (96, u16),
+    "code2": (96, f), "cU2": (96, u16), "tk": (96, f), "thr": (1, f), "f1": (96, b), "f2": (96, b),
+    "offA": (256, u16), "offZ": (192, u16), "failB": (256, b), "fail8": (256, b), "inv": (256, b), "QB": (512, b),
+    "nviol": (256, b), "cnt": (1, f), "failz": (192, b), "thi": (1, i32), "ai": (1, i32), "a3": (1, i32), "Tc": (1, f),
+    "Tb": (1, f), "diff": (128, f), "mj": (128, f), "vb": (128, b), "nvb": (128, b), "jx": (8, f), "jy": (8, f),
+    "jc": (8, u16), "km": (256, f), "ki": (16, i32), "ka": (16, i32), "kb": (16, b), "whi": (256, b), "wlo": (256, b),
+    "HL": (512, b), "litH": (16, f), "litL": (16, f), "litU": (16, u16), "us": (256, b), "UP": (512, b), "ng": (16, f),
+    "vL": (16, f), "vM": (16, f), "vN": (16, f), "vQ": (16, f), "y": (32, f), "cm": (16, f), "cN": (16, f), "nr": (256, f),
+    "vr": (256, f), "vU": (256, u16), "mv": (256, b), "o1": (32, f), "o2": (32, f), "oU": (32, u16),
+    "SW0": (400, f), "SW1": (400, f), "SW2": (400, f),
+    "pci": (1, i32), "pmi": (1, i32), "pgi": (1, i32), "pc": (1, f), "pm": (1, f), "pg16": (1, f), "k15": (1, f), "pg": (1, f),
+    "p16": (1, f), "row": (144, f), "grow": (128, f), "mrow": (128, f), "Blk": (128, b), "Eye": (128, b), "t1": (128, b),
+    "t2": (128, b), "t3": (128, b), "t4": (128, b), "t5": (128, b), "NTB": (128, b), "NI": (128, b), "Zw": (144, b),
+    "Zn": (144, b), "Zs": (144, b), "Z16": (144, b), "BC": (2048, b), "LT": (2048, b), "RM": (16, f), "LM": (16, f),
+    "r16": (16, f), "q8": (256, f), "K15": (256, b), "RST": (256, b), "J129": (128, b), "du": (32, f), "dum": (32, f),
+    "one": (128, b), "o16": (128, f), "kk": (256, f),
+}
+SCRATCH = {n: ("sbuf", [128, w], d) for n, (w, d) in BUFS.items()}
+SCRATCH.update({"FI": ("sbuf", [8, 1536], i32), "FB": ("sbuf", [8, 1536], b), "Z8": ("sbuf", [8, 144], b), "YF": ("sbuf", [8, 1536], f)})
+PSUM = ["p%d" % n for n in range(8)]
+SCRATCH.update({n: ("psum", [128, 512], f) for n in PSUM})
+SEMAPHORES = ["cv", "cs", "ct", "cg", "snd", "arr0", "arr1", "arr2"] + ["d%d" % n for n in range(8)]
+
+
+def tracker(g, T):
+    eng = {"v": g.vector, "s": g.scalar, "t": g.tensor, "g": g, "y": g.sync}
+    cnt, known, snap, hist, dmas = {}, {q: {} for q in eng}, {}, {}, [0]
+
+    def over(a, c):
+        if a[1] <= c[0] or c[1] <= a[0]:
+            return False
+        if a[2] == c[2] and a[2] > 1:
+            return a[0] % a[2] == c[0] % c[2]
+        return True
+
+    def clash(rec, reg, isw, q, buf):
+        if buf in PSUM and rec[2] != q:
+            return True
+        if not (isw or rec[1]) or not over(rec[0], reg):
+            return False
+        return rec[2] != q or q != "t"
+
+    def wait(q, sem, val):
+        if known[q].get(sem, 0) >= val:
+            return
+        eng[q].wait_ge(T.sem[sem], val)
+        for k, n in snap.get((sem, val), {}).items():
+            known[q][k] = max(known[q].get(k, 0), n)
+        known[q][sem] = max(known[q].get(sem, 0), val)
+
+    def note(q, tok, reads, writes):
+        snap[tok] = dict(known[q]) if q in known else {}
+        rq = q if tok[0][0] == "c" else tok[0]
+        for o, isw in [(o, False) for o in reads] + [(o, True) for o in writes]:
+            buf, reg = o[0], o[1:4]
+            h = hist.setdefault(buf, [])
+            if isw and reg[2] == 1:
+                h[:] = [r for r in h if not (reg[0] <= r[0][0] and r[0][1] <= reg[1])]
+            else:
+                h[:] = [r for r in h if not (r[0] == reg and r[2] == rq and r[1] == isw)]
+            h.append((reg, isw, rq, tok))
+
+    def need(q, reads, writes, rq):
+        ws = {}
+        for o, isw in [(o, False) for o in reads] + [(o, True) for o in writes]:
+            for r in hist.get(o[0], []):
+                if clash(r, o[1:4], isw, rq, o[0]):
+                    ws[r[3][0]] = max(ws.get(r[3][0], 0), r[3][1])
+        for s in sorted(ws):
+            wait(q, s, ws[s])
+
+    def run(q, fn, reads, writes):
+        need(q, reads, writes, q)
+        cnt[q] = cnt.get(q, 0) + 1
+        fn().then_inc(T.sem["c" + q], 1)
+        note(q, ("c" + q, cnt[q]), reads, writes)
+
+    def dma(q, out, in_, reads, writes):
+        need(q, reads, writes, "x")
+        n = "d%d" % dmas[0]
+        dmas[0] += 1
+        eng[q].dma_start(out, in_).then_inc(T.sem[n], 16)
+        note(q, (n, 16), reads, writes)
+
+    def finish(more):
+        for q in cnt:
+            wait("g", "c" + q, cnt[q])
+        for n in range(dmas[0]):
+            wait("g", "d%d" % n, 16)
+        for s, v in more:
+            wait("g", s, v)
+
+    return run, dma, need, note, wait, finish
+
+
+def rank_program(g, core, T, topo):
+    rank = T.rank_of(core)
+    if rank is None:
+        return
+    run, dma, need, note, wait, finish = tracker(g, T)
+    N = len(T.cores)
+    X = AF.Copy
+
+    def R(buf, c0=0, c1=None, st=1, P=None):
+        c1 = SCRATCH[buf][1][1] if c1 is None else c1
+        return (buf, c0, c1, st, P)
+
+    def col(buf, c):
+        return R(buf, c, c + 1)
+
+    def ap(o):
+        if len(o) == 2:
+            return ap(o[0]).indirect(ap(o[1]))
+        t = T[o[0]]
+        if o[4]:
+            return t[:o[4], o[1]:o[2]:o[3]] if o[3] > 1 else t[:o[4], o[1]:o[2]]
+        return t[:, o[1]:o[2]:o[3]] if o[3] > 1 else t[:, o[1]:o[2]]
+
+    def val(x):
+        return ap(x) if isinstance(x, tuple) else x
+
+    def rd(*xs):
+        r = []
+        for x in xs:
+            if isinstance(x, tuple):
+                r += list(x) if len(x) == 2 else [x]
+        return r
+
+    def wr(o):
+        return ([o[0]], [o[1]]) if len(o) == 2 else ([o], [])
+
+    def tt(out, a, c, op):
+        w, m = wr(out)
+        run("v", lambda: g.vector.tensor_tensor(out=ap(out), in0=ap(a), in1=ap(c), op=op), rd(a, c) + m, w)
+
+    def ts(out, a, s1, op0, s2=None, op1=None):
+        w, m = wr(out)
+        if op1 is None:
+            run("v", lambda: g.vector.tensor_scalar(out=ap(out), in0=ap(a), scalar1=val(s1), scalar2=None, op0=op0), rd(a, s1) + m, w)
+        else:
+            run("v", lambda: g.vector.tensor_scalar(out=ap(out), in0=ap(a), scalar1=val(s1), scalar2=val(s2), op0=op0, op1=op1), rd(a, s1, s2) + m, w)
+
+    def cp(out, a):
+        w, m = wr(out)
+        run("v", lambda: g.vector.tensor_copy(out=ap(out), in_=ap(a)), rd(a) + m, w)
+
+    def fill(o, c):
+        run("v", lambda: g.vector.memset(ap(o), c), [], [o])
+
+    def scan(out, d0, d1, init, op0, op1):
+        run("v", lambda: g.vector.tensor_tensor_scan(out=ap(out), data0=ap(d0), data1=ap(d1), initial=val(init), op0=op0, op1=op1), rd(d0, d1, init), [out])
+
+    def act(out, a, func=X, bias=0.0, scale=1.0, acc=None):
+        if acc is None:
+            run("s", lambda: g.scalar.activation(out=ap(out), in_=ap(a), func=func, bias=val(bias), scale=val(scale)), rd(a, bias, scale), [out])
+        else:
+            run("s", lambda: g.scalar.activation(out=ap(out), in_=ap(a), func=func, bias=val(bias), scale=val(scale), accum_out=ap(acc)), rd(a, bias, scale), [out, acc])
+
+    def mm(out, lhsT, rhs, start, stop):
+        run("t", lambda: g.tensor.matmul(out=ap(out), lhsT=ap(lhsT), rhs=ap(rhs), start=start, stop=stop), rd(lhsT, rhs), [out])
+
+    def chain(out, pairs, start=True, stop=True):
+        for n, (l, r) in enumerate(pairs):
+            mm(out, l, r, start and n == 0, stop and n == len(pairs) - 1)
+
+    def iota(o, pattern, base, cm):
+        if SCRATCH[o[0]][2] != i32:
+            run("g", lambda: g.iota(ap(o), pattern, base, cm, allow_small_or_imprecise_dtypes=True), [], [o])
+        else:
+            run("g", lambda: g.iota(ap(o), pattern, base, cm), [], [o])
+
+    def Z(buf, i):
+        return R(buf, 16 - i, 144 - i)
+
+    def tolist(out, x, n):
+        chain(out, [(Z("Zs", i), R(x, i, n, 16)) for i in range(16)])
+
+    dma("y", T.FI[:, :], T.fr[:, :], [], [R("FI")])
+    dma("y", T.CLI[:, :], T.cl[:, :], [], [R("CLI")])
+    dma("y", T.S[:, 0:3072], T.xv[:, :], [], [R("S", 0, 3072)])
+    dma("y", T.thi[:, :], T.th[:, :], [], [R("thi")])
+
+    iota(R("pci"), [[0, 1]], 0, 1)
+    iota(R("row"), [[1, 144]], -16, 0)
+    iota(R("grow"), [[1, 8], [0, 16]], 0, 0)
+    iota(R("mrow"), [[0, 8], [1, 16]], 0, 0)
+    iota(R("r16"), [[1, 16]], 0, 0)
+    iota(R("q8"), [[1, 256]], int(BIG), 0)
+    iota(R("W", 0, 256), [[0, 256]], 0, 0)
+    iota(R("W", BZ, BZ + 192), [[0, 192]], 0, 0)
+    for t in range(3):
+        iota(R("SW%d" % t, 0, RW), [[0, RW]], 0, 0)
+    iota(R("J129"), [[1, 128]], 129, 0)
+    iota(R("kk"), [[0, 16], [1, 16]], 0, 0)
+    iota(R("K15"), [[0, 16], [-1, 16]], 15, 0)
+    iota(R("du"), [[16, 32]], 6144, 0)
+    iota(R("VD"), [[0, 4608]], 8, 0)
+    ts(R("pmi"), R("pci"), 15, O.bitwise_and)
+    ts(R("pgi"), R("pci"), 4, O.arith_shift_right)
+    cp(R("pc"), R("pci"))
+    cp(R("pm"), R("pmi"))
+    cp(R("pg"), R("pgi"))
+    ts(R("p16"), R("pc"), 16.0, O.mult)
+    ts(R("pg16"), R("pg"), 16.0, O.mult)
+    ts(R("Blk"), R("grow"), col("pg", 0), O.is_equal)
+    ts(R("Eye"), R("row", 16, 144), col("pc", 0), O.is_equal)
+    ts(R("Z8"), R("row", P=8), R("p16", P=8), O.is_equal)
+    ts(R("RM"), R("r16"), col("pm", 0), O.is_equal)
+    ts(R("LM"), R("r16"), col("pm", 0), O.is_gt)
+    ts(R("t1"), R("mrow"), col("pm", 0), O.is_le, -1.0, O.mult)
+    ts(R("t2"), R("Eye"), -BIG - 1.0, O.mult)
+    cp(R("FB"), R("FI"))
+    chain(R("p0", 0, 96), [(R("Z8", 16 - i, 144 - i), R("FB", i, 1536, 16)) for i in range(16)])
+    ts(R("t3"), R("Eye"), -1.0, O.mult, 1.0, O.add)
+    tt(R("t4"), R("t1"), R("Blk"), O.mult)
+    fill(R("one"), 1.0)
+    tt(R("t5"), R("t4"), R("t3"), O.mult)
+    ts(R("NI"), R("Eye"), -32.0, O.mult)
+    tt(R("NTB"), R("t5"), R("t2"), O.add)
+    ts(R("Zw"), R("row"), col("pg16", 0), O.is_equal)
+    ts(R("k15"), R("pm"), -1.0, O.mult, 15.0, O.add)
+    cp(R("F"), R("p0", 0, 96))
+    act(R("S", 3072, 4608), R("S", 0, 1536), AF.Identity, 63.0, -1.0)
+    for i in range(16):
+        act(R("BC", 128 * i, 128 * i + 128), R("Blk"), X, 0.0, col("RM", i))
+    for i in range(1, 16):
+        act(R("LT", 128 * i, 128 * i + 128), R("Blk"), X, 0.0, col("LM", i))
+
+    def consts():
+        ts(R("Zs"), R("Zw"), 0.0625, O.mult)
+        ts(R("Zn"), R("Zw"), -1.0, O.mult)
+        cp(R("Tc"), R("thi"))
+        ts(R("Z16"), R("Zw"), 16.0, O.mult)
+        ts(R("Tb"), R("Tc"), -1.0, O.mult, 1.0, O.add)
+
+    def late_consts():
+        ts(R("S", 4608, 6144), R("S", 1536, 3072), -1.0, O.mult, 63.0, O.add)
+        ts(R("RST"), R("kk"), 0.5, O.is_gt)
+        ts(R("dum"), R("du"), col("pm", 0), O.add)
+        fill(R("o16"), 0.0625)
+
+    def flags():
+        ts(R("FL", 0, 96), R("F"), 0.0, O.is_equal)
+        ts(R("FL", 192, 288), R("F"), 4.0, O.is_ge)
+        ts(R("g1"), R("F"), 1.0, O.is_ge)
+        tt(R("FL", 96, 192), R("g1"), R("FL", 192, 288), O.subtract)
+
+    def counts():
+        mm(R("p1", 0, 288), R("Blk"), R("FL"), True, True)
+        mm(R("p0", 0, 288), R("NTB"), R("FL"), True, True)
+
+    def codes(t):
+        u = {0: 16 * t, 1: 32 * t, 2: 0}
+        for c, base in ((0, BA), (1, BZ), (2, BD)):
+            o = 96 * c
+            scan(R("IL", o + u[c], o + 96), R("one", u[c], 96), R("p1", o + u[c], o + 96), BIG + base, O.mult, O.add)
+        for c in (0, 1):
+            o = 96 * c
+            if u[c]:
+                scan(R("IL", o, o + u[c]), R("one", 0, u[c]), R("p1", o, o + u[c]), col("IL", o + 95), O.mult, O.add)
+        tt(R("rz"), R("IL"), R("p0", 0, 288), O.add)
+        tt(R("m1"), R("rz", 0, 96), R("rz", 96, 192), O.min)
+        tt(R("code"), R("m1"), R("rz", 192, 288), O.min)
+        cp(R("cU"), R("code"))
+
+    def pack(t):
+        ts(R("inv"), R("q8"), col("IL", (16 * t or 96) - 1), O.is_ge)
+        cp((R("W", 0, 4608), R("cU")), R("CLI" if t == 0 else "CLF"))
+
+    flags()
+    counts()
+    consts()
+    codes(0)
+    late_consts()
+    pack(0)
+
+    for t in range(3):
+        more = t < 2
+        base = BR + RW * t
+        sw = "SW%d" % t
+        TAB = R("S", 0, 6144)
+
+        def indicate(a0, a1):
+            ts(R("ind", 16 * a0, 16 * a1), R("s", 16 * a0, 16 * a1), col("Tc", 0), O.is_ge)
+            chain(R("p2", a0, a1), [(R("Eye"), R("ind", 16 * a0 + k, 16 * a1, 16)) for k in range(16)])
+
+        def tots(a0, a1):
+            chain(R("p4", a0 // 2, a1 // 2), [(Z(z, k), R("s", 16 * a0 + o + k, 16 * a1, 32)) for z, o in (("Zw", 16), ("Zn", 0)) for k in range(16)])
+
+        def planes(a0, a1, k0=0, k1=16):
+            for k in range(k0, k1):
+                tt(R("pr", 16 * a0 + k, 16 * a1, 16), R("s", 16 * a0 + k, 16 * a1, 16), R("p2", 256 + a0, 256 + a1), O.mult)
+
+        def sums(a0, a1):
+            chain(R("p6", 0, 256), [(Z("Z16", i), R("pr", 256 * i, 256 * i + 256)) for i in range(a0 // 16, a1 // 16)], False, a1 == 256)
+
+        cp(R("offA"), R("W", 0, 256))
+        cp(R("s", 0, 16 * A1), (TAB, R("offA", 0, A1)))
+        for a0, a1 in ((A1, A2), (A2, 256)):
+            act(R("s", 16 * a0, 16 * a1), (TAB, R("offA", a0, a1)))
+        cp(R("offZ"), R("W", BZ, BZ + 192))
+        for z0, z1 in ((0, 96), (96, 192)):
+            act(R("indz", 16 * z0, 16 * z1), (TAB, R("offZ", z0, z1)), AF.Relu, col("Tb", 0))
+        indicate(0, A1)
+        cp(R("whi"), R("W", 0, 256))
+        tt(R("diff"), R("W", 1, 256, 2), R("W", 0, 256, 2), O.subtract)
+        indicate(A1, A2)
+        tots(0, 128)
+        tt(R("wlo"), R("W", 0, 256), R("whi"), O.subtract)
+        indicate(A2, 256)
+        ts(R("failB"), R("p2", 0, 256), 0.5, O.is_lt)
+        chain(R("p3", 0, 256), [(R("NI"), R("inv")), (R("Blk"), R("failB"))])
+        tots(128, 256)
+        ts(R("p2", 256, 512), R("p2", 0, 256), 0.5, O.is_lt)
+        planes(0, 128, 0, 4)
+        ts(R("QB", 256, 512), R("p3", 0, 256), 5.5, O.is_gt)
+        tt(R("vb"), R("QB", 256, 512, 2), R("QB", 257, 512, 2), O.mult)
+        planes(0, 128, 4, 5)
+        scan(R("QB", 0, 128), R("one"), R("vb"), 0.0, O.mult, O.add)
+        ts(R("nvb"), R("vb"), 0.5, O.is_lt)
+        planes(0, 128, 5, 6)
+        tt(R("QB", 128, 256), R("nvb"), R("J129"), O.mult)
+        tolist(R("p3", 256, 288), "QB", 512)
+        planes(0, 128, 6, 10)
+        ts(R("p4", 128, 256), R("p4", 0, 128), 0.0, O.is_gt)
+        planes(0, 128, 10, 11)
+        tt(R("mj"), R("diff"), R("p4", 128, 256), O.mult)
+        cp(R("jx"), R("p3", 256, 264))
+        planes(0, 128, 11, 12)
+        tt(R("jy"), R("jx"), R("p3", 264, 272), O.add)
+        cp(R(sw, 0, 1), R("QB", 127, 128))
+        planes(0, 128, 12, 13)
+        cp(R("jc"), R("jy"))
+        planes(0, 128, 13, 14)
+        tt((R(sw), R("jc")), R("mj"), R("W", 0, 256, 2), O.add)
+        dst = T.cores[(rank + 1 + t) % N]
+        src = T.cores[(rank - 1 - t) % N]
+        need("g", [R(sw, 0, RW)], [], "x")
+        rid, pid, _ = topo.addr(dst)
+        g.remote_dma(T.W[:, base:base + RW], T[sw][:, 0:RW], T.sem["arr%d" % t], T.sem.snd, pid, rid, sum(1 << e for e in topo.engines(core, dst)[::2]))
+        note("rem", ("arr%d" % t, len(topo.engines(src, core)[::2])), [], [R("W", base, base + RW)])
+        planes(0, 128, 14, 16)
+        mm(R("p6", 0, 256), R("Eye"), R("K15"), True, False)
+        sums(0, 128)
+        chain(R("p5", 0, 96), [(R("Eye"), R("indz", k, 1536, 16)) for k in range(16)])
+        planes(128, 192)
+        sums(128, 192)
+        chain(R("p5", 96, 192), [(R("Eye"), R("indz", 1536 + k, 3072, 16)) for k in range(16)])
+        act(R("nviol"), R("QB", 256, 512), AF.Identity, 1.0, -1.0, R("cnt"))
+        act(R("VD", 0, 256), R("QB", 256, 512), AF.Identity, 9.0, -1.0)
+        act(R("fail8"), R("failB"), X, 0.0, 8.0)
+        planes(192, 256)
+        ts(R("failz"), R("p5", 0, 192), 0.5, O.is_lt)
+        mm(R("p5", 256, 448), R("Blk"), R("failz"), True, True)
+        sums(192, 256)
+        ts(R("VD", BZ, BZ + 192), R("p5", 256, 448), 5.5, O.is_le, 9.0, O.mult)
+        act(R("DR"), (R("VD"), R("cU")))
+        scan(R("km"), R("RST"), R("p6", 0, 256), 0.0, O.mult, O.max)
+        cp(R("ki"), R("km", 15, 256, 16))
+        ts(R("ka"), R("ki"), 15, O.bitwise_and)
+        cp(R("kb"), R("ka"))
+        for i in range(16):
+            mm(R("p6", 16 * i, 16 * i + 16), R("BC", 128 * i, 128 * i + 128), R("kb"), True, True)
+        ts(R("thr"), R("W", base, base + 1), float(BD), O.add)
+        ts(R("tk"), R("rz", 192, 288), col("thr", 0), O.is_lt, float(base + 1 - BD), O.mult)
+        tt(R("code2"), R("code"), R("tk"), O.add)
+        cp(R("cU2"), R("code2"))
+        act(R("CLF"), (R("W", 0, base + RW), R("cU2")))
+        ts(R("p6", 256, 512), R("p6", 0, 256), col("k15", 0), O.is_equal)
+        tt(R("HL", 0, 256), R("whi"), R("p6", 256, 512), O.mult)
+        tt(R("HL", 256, 512), R("wlo"), R("p6", 256, 512), O.mult)
+        chain(R("p7", 0, 256), [(R("Blk"), R("HL", 0, 256)), (R("Blk"), R("HL", 256, 512))])
+        chain(R("p0", 288, 320), [(Z("Zw", i), R("HL", i, 512, 16)) for i in range(16)])
+        tolist(R("p5", 0, 96), "DR", 1536)
+        ts(R("nr"), R("p7", 0, 256), 3072.0, O.is_ge, -3072.0, O.mult)
+        tt(R("vr"), R("nr"), R("p7", 0, 256), O.add)
+        cp(R("litH"), R("p0", 288, 304))
+        cp(R("vU"), R("vr"))
+        tt(R("litL"), R("litH"), R("p0", 304, 320), O.add)
+        ts(R("ng"), R("litL"), 3072.0, O.is_ge, -3072.0, O.mult)
+        cp(R("litU"), R("litL"))
+        tt(R("vL"), R("litL"), R("ng"), O.add)
+        ts(R("vM"), R("vL"), 1.0, O.add)
+        tt(R("vN"), R("vM"), R("p3", 272, 288), O.mult)
+        ts(R("vQ"), R("vN"), -1.0, O.add)
+        for c in range(16):
+            ts(R("E", 272 * c, 256 * c + 256), R("vU", 16 * c, 256), col("vQ", c), O.is_equal)
+        mm(R("p4", 0, 256), R("Eye"), R("nviol"), True, False)
+        for c in range(15):
+            mm(R("p4", 16 * c + 16, 256), R("Blk"), R("E", 272 * c + 16, 256 * c + 256), False, False)
+        tt(R("f1"), R("F"), R("p5", 0, 96), O.add)
+        tt(R("us"), (TAB, R("litU")), R("fail8"), O.add)
+        tt(R("f2"), R("f1"), R("tk"), O.subtract)
+        ts(R("UP", 0, 256), R("us"), 63.0, O.min)
+        ts(R("F"), R("f2"), -8.0, O.add, 0.0, O.max)
+        ts(R("UP", 256, 512), R("UP", 0, 256), -1.0, O.mult, 63.0, O.add)
+        if more:
+            flags()
+            counts()
+        for i in range(1, 16):
+            mm(R("p4", i, 256, 16), R("LT", 128 * i, 128 * i + 128), R("E", i, 4096, 272), False, False)
+        mm(R("p4", 0, 256), R("Eye"), R("nviol"), False, True)
+        tt(R("cm"), R("vL"), R("ng"), O.add)
+        tt(R("y", 0, 16), R("litL"), R("dum", 0, 16), O.subtract)
+        ts(R("cN"), R("cm"), 3072.0, O.add)
+        tt(R("y", 16, 32), R("cN"), R("dum", 16, 32), O.subtract)
+        if more:
+            codes(t + 1)
+            mm(R("p3", 300, 301), R("o16"), R("cnt"), True, True)
+        ts(R("mv"), R("p4", 0, 256), 0.5, O.is_lt)
+        tolist(R("p7", 256, 272), "mv", 256)
+        if more:
+            pack(t + 1)
+            ts(R("ai"), R("p3", 300, 301), -1.0, O.mult, 2048.0, O.add)
+        tt(R("o1", 0, 16), R("y", 0, 16), R("p7", 256, 272), O.mult)
+        tt(R("o1", 16, 32), R("y", 16, 32), R("p7", 256, 272), O.mult)
+        if more:
+            ts(R("a3"), R("ai"), 3, O.bitwise_and)
+        tt(R("o2"), R("o1"), R("dum"), O.add)
+        if more:
+            tt(R("Tc"), R("a3"), R("thi"), O.add)
+        cp(R("oU"), R("o2"))
+        if more:
+            ts(R("Tb"), R("Tc"), -1.0, O.mult, 1.0, O.add)
+        cp((R("S"), R("oU")), R("UP"))
+
+    dma("y", T.yc[:, :], T.CLF[:, :], [R("CLF")], [])
+    for c in range(3):
+        for i in range(16):
+            mm(R("p%d" % c, i, 512, 16, 8), R("BC", 128 * i, 128 * i + 128, 16), R("F", 32 * c, 32 * c + 32), True, True)
+        act(R("YF", 512 * c, 512 * c + 512), R("p%d" % c, 0, 512, 1, 8))
+    dma("y", T.yf[:, :], T.YF[:, :], [R("YF")], [])
+    dma("y", T.yx[:, :], T.S[:, 0:3072], [R("S", 0, 3072)], [])
+    sent = sum(len(topo.engines(core, T.cores[(rank + 1 + t) % N])[::2]) for t in range(3))
+    finish([("snd", sent)] + [("arr%d" % t, len(topo.engines(T.cores[(rank - 1 - t) % N], core)[::2])) for t in range(3)])

@@ -2,8 +2,10 @@ from concourse.mybir import AluOpType as O, ActivationFunctionType as AF
 
 BA, BZ, BD, BR, RW = 0, 1536, 3072, 4608, 132
 BIG = 8191.0
+MAGIC = 8388608.0
 A1, A2 = 80, 176
-PARTS = ((0, 128), (128, 192), (192, 256))
+SPL = 160
+ZC = 128
 f, b, i32, u16 = "float32", "bfloat16", "int32", "uint16"
 BUFS = {
     "S": (6656, b), "s": (4096, b), "ind": (4096, b), "indz": (3072, b), "pr": (4096, b), "W": (BR + 3 * RW, f),
@@ -23,7 +25,7 @@ BUFS = {
     "t2": (128, b), "t3": (128, b), "t4": (128, b), "t5": (128, b), "NTB": (128, b), "NI": (128, b), "Zw": (144, b),
     "Zn": (144, b), "Zs": (144, b), "Z16": (144, b), "BC": (2048, b), "LT": (2048, b), "RM": (16, f), "LM": (16, f),
     "r16": (16, f), "q8": (256, f), "K15": (256, b), "RST": (256, b), "J129": (128, b), "du": (32, f), "dum": (32, f),
-    "one": (128, b), "o16": (128, f), "kk": (256, f),
+    "one": (128, b), "E64": (128, b), "o16": (128, f), "kk": (256, f),
 }
 SCRATCH = {n: ("sbuf", [128, w], d) for n, (w, d) in BUFS.items()}
 SCRATCH.update({"FI": ("sbuf", [8, 1536], i32), "FB": ("sbuf", [8, 1536], b), "Z8": ("sbuf", [8, 144], b), "YF": ("sbuf", [8, 1536], f)})
@@ -161,7 +163,10 @@ def rank_program(g, core, T, topo):
         run("v", lambda: g.vector.tensor_tensor_scan(out=ap(out), data0=ap(d0), data1=ap(d1), initial=val(init), op0=op0, op1=op1), rd(d0, d1, init), [out])
 
     def act(out, a, func=X, bias=0.0, scale=1.0, acc=None):
-        if acc is None:
+        if len(out) == 2:
+            w, m = wr(out)
+            run("s", lambda: g.scalar.activation(out=ap(out), in_=ap(a), func=func), rd(a) + m, w)
+        elif acc is None:
             run("s", lambda: g.scalar.activation(out=ap(out), in_=ap(a), func=func, bias=val(bias), scale=val(scale)), rd(a, bias, scale), [out])
         else:
             run("s", lambda: g.scalar.activation(out=ap(out), in_=ap(a), func=func, bias=val(bias), scale=val(scale), accum_out=ap(acc)), rd(a, bias, scale), [out, acc])
@@ -248,6 +253,7 @@ def rank_program(g, core, T, topo):
         ts(R("RST"), R("kk"), 0.5, O.is_gt)
         ts(R("dum"), R("du"), col("pm", 0), O.add)
         fill(R("o16"), 0.0625)
+        ts(R("E64"), R("Eye"), 64.0, O.mult)
 
     def flags():
         ts(R("FL", 0, 96), R("F"), 0.0, O.is_equal)
@@ -275,7 +281,10 @@ def rank_program(g, core, T, topo):
 
     def pack(t):
         ts(R("inv"), R("q8"), col("IL", (16 * t or 96) - 1), O.is_ge)
-        cp((R("W", 0, 4608), R("cU")), R("CLI" if t == 0 else "CLF"))
+        if t == 0:
+            cp((R("W", 0, 4608), R("cU")), R("CLI"))
+        else:
+            act((R("W", 0, 4608), R("cU")), R("CLF"), AF.Silu)
 
     flags()
     counts()
@@ -287,6 +296,7 @@ def rank_program(g, core, T, topo):
     for t in range(3):
         more = t < 2
         base = BR + RW * t
+        add = 64.0 if t else 0.0
         sw = "SW%d" % t
         TAB = R("S", 0, 6144)
 
@@ -297,51 +307,66 @@ def rank_program(g, core, T, topo):
         def tots(a0, a1):
             chain(R("p4", a0 // 2, a1 // 2), [(Z(z, k), R("s", 16 * a0 + o + k, 16 * a1, 32)) for z, o in (("Zw", 16), ("Zn", 0)) for k in range(16)])
 
-        def planes(a0, a1, k0=0, k1=16):
+        def planes(k0, k1):
             for k in range(k0, k1):
-                tt(R("pr", 16 * a0 + k, 16 * a1, 16), R("s", 16 * a0 + k, 16 * a1, 16), R("p2", 256 + a0, 256 + a1), O.mult)
+                tt(R("pr", k, 16 * SPL, 16), R("s", k, 16 * SPL, 16), R("p2", 256, 256 + SPL), O.mult)
 
-        def sums(a0, a1):
-            chain(R("p6", 0, 256), [(Z("Z16", i), R("pr", 256 * i, 256 * i + 256)) for i in range(a0 // 16, a1 // 16)], False, a1 == 256)
+        def relus():
+            w, n = 256 - SPL, 0
+            for k in range(16):
+                o = R(("p0", "p1", "p7", "p5")[k % 4], n, n + w)
+                n += w if k % 4 == 3 else 0
+                n = 0 if n + w > 512 else n
+                chain(o, [(R("Eye"), R("s", 16 * SPL + k, 4096, 16)), (R("E64"), R("failB", SPL, 256))])
+                act(R("pr", 16 * SPL + k, 4096, 16), o, AF.Relu, -64.0)
 
-        cp(R("offA"), R("W", 0, 256))
+        def sums(a0, a1, stop):
+            chain(R("p6", 0, 256), [(Z("Z16", i), R("pr", 256 * i, 256 * i + 256)) for i in range(a0 // 16, a1 // 16)], False, stop)
+
+        def frozen(z0, z1):
+            act(R("indz", 16 * z0, 16 * z1), (TAB, R("offZ", z0, z1)), AF.Relu, col("Tb", 0))
+
+        def frozen_sums(z0, z1):
+            chain(R("p5", z0, z1), [(R("Eye"), R("indz", 16 * z0 + k, 16 * z1, 16)) for k in range(16)])
+
+        ts(R("offA"), R("W", 0, 256), MAGIC, O.add, -MAGIC - add, O.add)
         cp(R("s", 0, 16 * A1), (TAB, R("offA", 0, A1)))
         for a0, a1 in ((A1, A2), (A2, 256)):
             act(R("s", 16 * a0, 16 * a1), (TAB, R("offA", a0, a1)))
-        cp(R("offZ"), R("W", BZ, BZ + 192))
-        for z0, z1 in ((0, 96), (96, 192)):
-            act(R("indz", 16 * z0, 16 * z1), (TAB, R("offZ", z0, z1)), AF.Relu, col("Tb", 0))
+        ts(R("offZ"), R("W", BZ, BZ + 192), MAGIC, O.add, -MAGIC - add, O.add)
+        frozen(0, ZC)
         indicate(0, A1)
-        cp(R("whi"), R("W", 0, 256))
+        tots(0, 128)
+        ts(R("whi"), R("W", 0, 256), -add, O.add)
         tt(R("diff"), R("W", 1, 256, 2), R("W", 0, 256, 2), O.subtract)
         indicate(A1, A2)
-        tots(0, 128)
         tt(R("wlo"), R("W", 0, 256), R("whi"), O.subtract)
         indicate(A2, 256)
         ts(R("failB"), R("p2", 0, 256), 0.5, O.is_lt)
         chain(R("p3", 0, 256), [(R("NI"), R("inv")), (R("Blk"), R("failB"))])
         tots(128, 256)
         ts(R("p2", 256, 512), R("p2", 0, 256), 0.5, O.is_lt)
-        planes(0, 128, 0, 4)
+        relus()
+        planes(0, 4)
         ts(R("QB", 256, 512), R("p3", 0, 256), 5.5, O.is_gt)
         tt(R("vb"), R("QB", 256, 512, 2), R("QB", 257, 512, 2), O.mult)
-        planes(0, 128, 4, 5)
+        planes(4, 5)
         scan(R("QB", 0, 128), R("one"), R("vb"), 0.0, O.mult, O.add)
         ts(R("nvb"), R("vb"), 0.5, O.is_lt)
-        planes(0, 128, 5, 6)
+        planes(5, 6)
         tt(R("QB", 128, 256), R("nvb"), R("J129"), O.mult)
         tolist(R("p3", 256, 288), "QB", 512)
-        planes(0, 128, 6, 10)
+        planes(6, 10)
         ts(R("p4", 128, 256), R("p4", 0, 128), 0.0, O.is_gt)
-        planes(0, 128, 10, 11)
+        planes(10, 11)
         tt(R("mj"), R("diff"), R("p4", 128, 256), O.mult)
         cp(R("jx"), R("p3", 256, 264))
-        planes(0, 128, 11, 12)
+        planes(11, 12)
         tt(R("jy"), R("jx"), R("p3", 264, 272), O.add)
         cp(R(sw, 0, 1), R("QB", 127, 128))
-        planes(0, 128, 12, 13)
+        planes(12, 13)
         cp(R("jc"), R("jy"))
-        planes(0, 128, 13, 14)
+        planes(13, 14)
         tt((R(sw), R("jc")), R("mj"), R("W", 0, 256, 2), O.add)
         dst = T.cores[(rank + 1 + t) % N]
         src = T.cores[(rank - 1 - t) % N]
@@ -349,48 +374,56 @@ def rank_program(g, core, T, topo):
         rid, pid, _ = topo.addr(dst)
         g.remote_dma(T.W[:, base:base + RW], T[sw][:, 0:RW], T.sem["arr%d" % t], T.sem.snd, pid, rid, sum(1 << e for e in topo.engines(core, dst)[::2]))
         note("rem", ("arr%d" % t, len(topo.engines(src, core)[::2])), [], [R("W", base, base + RW)])
-        planes(0, 128, 14, 16)
-        mm(R("p6", 0, 256), R("Eye"), R("K15"), True, False)
-        sums(0, 128)
-        chain(R("p5", 0, 96), [(R("Eye"), R("indz", k, 1536, 16)) for k in range(16)])
-        planes(128, 192)
-        sums(128, 192)
-        chain(R("p5", 96, 192), [(R("Eye"), R("indz", 1536 + k, 3072, 16)) for k in range(16)])
-        act(R("nviol"), R("QB", 256, 512), AF.Identity, 1.0, -1.0, R("cnt"))
+        frozen(ZC, 192)
         act(R("VD", 0, 256), R("QB", 256, 512), AF.Identity, 9.0, -1.0)
-        act(R("fail8"), R("failB"), X, 0.0, 8.0)
-        planes(192, 256)
+        planes(14, 16)
+        frozen_sums(0, ZC)
+        mm(R("p6", 0, 256), R("Eye"), R("K15"), True, False)
+        sums(SPL, 256, False)
+        frozen_sums(ZC, 192)
+        sums(0, 48, False)
         ts(R("failz"), R("p5", 0, 192), 0.5, O.is_lt)
         mm(R("p5", 256, 448), R("Blk"), R("failz"), True, True)
-        sums(192, 256)
+        sums(48, SPL, True)
         ts(R("VD", BZ, BZ + 192), R("p5", 256, 448), 5.5, O.is_le, 9.0, O.mult)
         act(R("DR"), (R("VD"), R("cU")))
+        act(R("nviol"), R("QB", 256, 512), AF.Identity, 1.0, -1.0, R("cnt"))
+        act(R("fail8"), R("failB"), X, 0.0, 8.0)
         scan(R("km"), R("RST"), R("p6", 0, 256), 0.0, O.mult, O.max)
         cp(R("ki"), R("km", 15, 256, 16))
         ts(R("ka"), R("ki"), 15, O.bitwise_and)
         cp(R("kb"), R("ka"))
         for i in range(16):
             mm(R("p6", 16 * i, 16 * i + 16), R("BC", 128 * i, 128 * i + 128), R("kb"), True, True)
+        ts(R("p6", 256, 512), R("p6", 0, 256), col("k15", 0), O.is_equal)
+        tt(R("HL", 0, 256), R("whi"), R("p6", 256, 512), O.mult)
+        tt(R("HL", 256, 512), R("wlo"), R("p6", 256, 512), O.mult)
         ts(R("thr"), R("W", base, base + 1), float(BD), O.add)
         ts(R("tk"), R("rz", 192, 288), col("thr", 0), O.is_lt, float(base + 1 - BD), O.mult)
         tt(R("code2"), R("code"), R("tk"), O.add)
         cp(R("cU2"), R("code2"))
-        act(R("CLF"), (R("W", 0, base + RW), R("cU2")))
-        ts(R("p6", 256, 512), R("p6", 0, 256), col("k15", 0), O.is_equal)
-        tt(R("HL", 0, 256), R("whi"), R("p6", 256, 512), O.mult)
-        tt(R("HL", 256, 512), R("wlo"), R("p6", 256, 512), O.mult)
-        chain(R("p7", 0, 256), [(R("Blk"), R("HL", 0, 256)), (R("Blk"), R("HL", 256, 512))])
-        chain(R("p0", 288, 320), [(Z("Zw", i), R("HL", i, 512, 16)) for i in range(16)])
+        act(R("CLF"), (R("W", 0, base + RW), R("cU2")), AF.Identity, (64.0, 0.0, MAGIC - 64.0)[t])
         tolist(R("p5", 0, 96), "DR", 1536)
-        ts(R("nr"), R("p7", 0, 256), 3072.0, O.is_ge, -3072.0, O.mult)
+        tt(R("f1"), R("F"), R("p5", 0, 96), O.add)
+        tt(R("f2"), R("f1"), R("tk"), O.subtract)
+        ts(R("F"), R("f2"), -8.0, O.add, 0.0, O.max)
+        chain(R("p7", 0, 256), [(R("Blk"), R("HL", 0, 256)), (R("Blk"), R("HL", 256, 512))])
+        chain(R("p2", 0, 32), [(Z("Zw", i), R("HL", i, 512, 16)) for i in range(16)])
+        if more:
+            flags()
+            counts()
+        ts(R("nr"), R("p7", 0, 256), 3071.5 + add, O.is_ge, -3072.0, O.mult)
+        ts(R("litH"), R("p2", 0, 16), MAGIC, O.add, -MAGIC - add, O.add)
         tt(R("vr"), R("nr"), R("p7", 0, 256), O.add)
-        cp(R("litH"), R("p0", 288, 304))
-        cp(R("vU"), R("vr"))
-        tt(R("litL"), R("litH"), R("p0", 304, 320), O.add)
+        tt(R("litL"), R("litH"), R("p2", 16, 32), O.add)
+        if more:
+            codes(t + 1)
+            pack(t + 1)
+        ts(R("vU"), R("vr"), MAGIC, O.add, -MAGIC, O.add)
         ts(R("ng"), R("litL"), 3072.0, O.is_ge, -3072.0, O.mult)
         cp(R("litU"), R("litL"))
         tt(R("vL"), R("litL"), R("ng"), O.add)
-        ts(R("vM"), R("vL"), 1.0, O.add)
+        ts(R("vM"), R("vL"), 1.0 + add, O.add)
         tt(R("vN"), R("vM"), R("p3", 272, 288), O.mult)
         ts(R("vQ"), R("vN"), -1.0, O.add)
         for c in range(16):
@@ -398,29 +431,21 @@ def rank_program(g, core, T, topo):
         mm(R("p4", 0, 256), R("Eye"), R("nviol"), True, False)
         for c in range(15):
             mm(R("p4", 16 * c + 16, 256), R("Blk"), R("E", 272 * c + 16, 256 * c + 256), False, False)
-        tt(R("f1"), R("F"), R("p5", 0, 96), O.add)
         tt(R("us"), (TAB, R("litU")), R("fail8"), O.add)
-        tt(R("f2"), R("f1"), R("tk"), O.subtract)
+        tt(R("cm"), R("vL"), R("ng"), O.add)
         ts(R("UP", 0, 256), R("us"), 63.0, O.min)
-        ts(R("F"), R("f2"), -8.0, O.add, 0.0, O.max)
+        ts(R("cN"), R("cm"), 3072.0, O.add)
         ts(R("UP", 256, 512), R("UP", 0, 256), -1.0, O.mult, 63.0, O.add)
-        if more:
-            flags()
-            counts()
         for i in range(1, 16):
             mm(R("p4", i, 256, 16), R("LT", 128 * i, 128 * i + 128), R("E", i, 4096, 272), False, False)
         mm(R("p4", 0, 256), R("Eye"), R("nviol"), False, True)
-        tt(R("cm"), R("vL"), R("ng"), O.add)
         tt(R("y", 0, 16), R("litL"), R("dum", 0, 16), O.subtract)
-        ts(R("cN"), R("cm"), 3072.0, O.add)
         tt(R("y", 16, 32), R("cN"), R("dum", 16, 32), O.subtract)
         if more:
-            codes(t + 1)
             mm(R("p3", 300, 301), R("o16"), R("cnt"), True, True)
         ts(R("mv"), R("p4", 0, 256), 0.5, O.is_lt)
         tolist(R("p7", 256, 272), "mv", 256)
         if more:
-            pack(t + 1)
             ts(R("ai"), R("p3", 300, 301), -1.0, O.mult, 2048.0, O.add)
         tt(R("o1", 0, 16), R("y", 0, 16), R("p7", 256, 272), O.mult)
         tt(R("o1", 16, 32), R("y", 16, 32), R("p7", 256, 272), O.mult)
@@ -434,6 +459,7 @@ def rank_program(g, core, T, topo):
             ts(R("Tb"), R("Tc"), -1.0, O.mult, 1.0, O.add)
         cp((R("S"), R("oU")), R("UP"))
 
+    act(R("CLF"), R("CLF"), AF.Identity, -MAGIC)
     dma("y", T.yc[:, :], T.CLF[:, :], [R("CLF")], [])
     for c in range(3):
         for i in range(16):

from concourse.mybir import AluOpType as O, ActivationFunctionType as AF

BA, BZ, BD, BR, RW = 0, 1536, 3072, 4608, 132
BIG = 8191.0
MAGIC = 8388608.0
A1, A2 = 80, 176
SPL = 160
ZC = 128
f, b, i32, u16 = "float32", "bfloat16", "int32", "uint16"
BUFS = {
    "S": (6656, b), "s": (4096, b), "ind": (4096, b), "indz": (3072, b), "pr": (4096, b), "W": (BR + 3 * RW, f),
    "CLI": (1536, i32), "CLF": (1536, f), "VD": (4608, b), "DR": (1536, b), "E": (4096, b), "F": (96, b),
    "FL": (288, b), "g1": (96, b), "IL": (288, f), "rz": (288, f), "m1": (96, f), "code": (96, f), "cU": (96, u16),
    "code2": (96, f), "cU2": (96, u16), "tk": (96, f), "thr": (1, f), "f1": (96, b), "f2": (96, b),
    "offA": (256, u16), "offZ": (192, u16), "failB": (256, b), "fail8": (256, b), "inv": (256, b), "QB": (512, b),
    "nviol": (256, b), "cnt": (1, f), "failz": (192, b), "thi": (1, i32), "ai": (1, i32), "a3": (1, i32), "Tc": (1, f),
    "Tb": (1, f), "diff": (128, f), "mj": (128, f), "vb": (128, b), "nvb": (128, b), "jx": (8, f), "jy": (8, f),
    "jc": (8, u16), "km": (256, f), "ki": (16, i32), "ka": (16, i32), "kb": (16, b), "whi": (256, b), "wlo": (256, b),
    "HL": (512, b), "litH": (16, f), "litL": (16, f), "litU": (16, u16), "us": (256, b), "UP": (512, b), "ng": (16, f),
    "vL": (16, f), "vM": (16, f), "vN": (16, f), "vQ": (16, f), "y": (32, f), "cm": (16, f), "cN": (16, f), "nr": (256, f),
    "vr": (256, f), "vU": (256, u16), "mv": (256, b), "o1": (32, f), "o2": (32, f), "oU": (32, u16),
    "SW0": (400, f), "SW1": (400, f), "SW2": (400, f),
    "pci": (1, i32), "pmi": (1, i32), "pgi": (1, i32), "pc": (1, f), "pm": (1, f), "pg16": (1, f), "k15": (1, f), "pg": (1, f),
    "p16": (1, f), "row": (144, f), "grow": (128, f), "mrow": (128, f), "Blk": (128, b), "Eye": (128, b), "t1": (128, b),
    "t2": (128, b), "t3": (128, b), "t4": (128, b), "t5": (128, b), "NTB": (128, b), "NI": (128, b), "Zw": (144, b),
    "Zn": (144, b), "Zs": (144, b), "Z16": (144, b), "BC": (2048, b), "LT": (2048, b), "RM": (16, f), "LM": (16, f),
    "r16": (16, f), "q8": (256, f), "K15": (256, b), "RST": (256, b), "J129": (128, b), "du": (32, f), "dum": (32, f),
    "one": (128, b), "E64": (128, b), "o16": (128, f), "kk": (256, f),
}
SCRATCH = {n: ("sbuf", [128, w], d) for n, (w, d) in BUFS.items()}
SCRATCH.update({"FI": ("sbuf", [8, 1536], i32), "FB": ("sbuf", [8, 1536], b), "Z8": ("sbuf", [8, 144], b), "YF": ("sbuf", [8, 1536], f)})
PSUM = ["p%d" % n for n in range(8)]
SCRATCH.update({n: ("psum", [128, 512], f) for n in PSUM})
SEMAPHORES = ["cv", "cs", "ct", "cg", "snd", "arr0", "arr1", "arr2"] + ["d%d" % n for n in range(8)]


def tracker(g, T):
    eng = {"v": g.vector, "s": g.scalar, "t": g.tensor, "g": g, "y": g.sync}
    cnt, known, snap, hist, dmas = {}, {q: {} for q in eng}, {}, {}, [0]

    def over(a, c):
        if a[1] <= c[0] or c[1] <= a[0]:
            return False
        if a[2] == c[2] and a[2] > 1:
            return a[0] % a[2] == c[0] % c[2]
        return True

    def clash(rec, reg, isw, q, buf):
        if buf in PSUM and rec[2] != q:
            return True
        if not (isw or rec[1]) or not over(rec[0], reg):
            return False
        return rec[2] != q or q != "t"

    def wait(q, sem, val):
        if known[q].get(sem, 0) >= val:
            return
        eng[q].wait_ge(T.sem[sem], val)
        for k, n in snap.get((sem, val), {}).items():
            known[q][k] = max(known[q].get(k, 0), n)
        known[q][sem] = max(known[q].get(sem, 0), val)

    def note(q, tok, reads, writes):
        snap[tok] = dict(known[q]) if q in known else {}
        rq = q if tok[0][0] == "c" else tok[0]
        for o, isw in [(o, False) for o in reads] + [(o, True) for o in writes]:
            buf, reg = o[0], o[1:4]
            h = hist.setdefault(buf, [])
            if isw and reg[2] == 1:
                h[:] = [r for r in h if not (reg[0] <= r[0][0] and r[0][1] <= reg[1])]
            else:
                h[:] = [r for r in h if not (r[0] == reg and r[2] == rq and r[1] == isw)]
            h.append((reg, isw, rq, tok))

    def need(q, reads, writes, rq):
        ws = {}
        for o, isw in [(o, False) for o in reads] + [(o, True) for o in writes]:
            for r in hist.get(o[0], []):
                if clash(r, o[1:4], isw, rq, o[0]):
                    ws[r[3][0]] = max(ws.get(r[3][0], 0), r[3][1])
        for s in sorted(ws):
            wait(q, s, ws[s])

    def run(q, fn, reads, writes):
        need(q, reads, writes, q)
        cnt[q] = cnt.get(q, 0) + 1
        fn().then_inc(T.sem["c" + q], 1)
        note(q, ("c" + q, cnt[q]), reads, writes)

    def dma(q, out, in_, reads, writes):
        need(q, reads, writes, "x")
        n = "d%d" % dmas[0]
        dmas[0] += 1
        eng[q].dma_start(out, in_).then_inc(T.sem[n], 16)
        note(q, (n, 16), reads, writes)

    def finish(more):
        for q in cnt:
            wait("g", "c" + q, cnt[q])
        for n in range(dmas[0]):
            wait("g", "d%d" % n, 16)
        for s, v in more:
            wait("g", s, v)

    return run, dma, need, note, wait, finish


def rank_program(g, core, T, topo):
    rank = T.rank_of(core)
    if rank is None:
        return
    run, dma, need, note, wait, finish = tracker(g, T)
    N = len(T.cores)
    X = AF.Copy

    def R(buf, c0=0, c1=None, st=1, P=None):
        c1 = SCRATCH[buf][1][1] if c1 is None else c1
        return (buf, c0, c1, st, P)

    def col(buf, c):
        return R(buf, c, c + 1)

    def ap(o):
        if len(o) == 2:
            return ap(o[0]).indirect(ap(o[1]))
        t = T[o[0]]
        if o[4]:
            return t[:o[4], o[1]:o[2]:o[3]] if o[3] > 1 else t[:o[4], o[1]:o[2]]
        return t[:, o[1]:o[2]:o[3]] if o[3] > 1 else t[:, o[1]:o[2]]

    def val(x):
        return ap(x) if isinstance(x, tuple) else x

    def rd(*xs):
        r = []
        for x in xs:
            if isinstance(x, tuple):
                r += list(x) if len(x) == 2 else [x]
        return r

    def wr(o):
        return ([o[0]], [o[1]]) if len(o) == 2 else ([o], [])

    def tt(out, a, c, op):
        w, m = wr(out)
        run("v", lambda: g.vector.tensor_tensor(out=ap(out), in0=ap(a), in1=ap(c), op=op), rd(a, c) + m, w)

    def ts(out, a, s1, op0, s2=None, op1=None):
        w, m = wr(out)
        if op1 is None:
            run("v", lambda: g.vector.tensor_scalar(out=ap(out), in0=ap(a), scalar1=val(s1), scalar2=None, op0=op0), rd(a, s1) + m, w)
        else:
            run("v", lambda: g.vector.tensor_scalar(out=ap(out), in0=ap(a), scalar1=val(s1), scalar2=val(s2), op0=op0, op1=op1), rd(a, s1, s2) + m, w)

    def cp(out, a):
        w, m = wr(out)
        run("v", lambda: g.vector.tensor_copy(out=ap(out), in_=ap(a)), rd(a) + m, w)

    def fill(o, c):
        run("v", lambda: g.vector.memset(ap(o), c), [], [o])

    def scan(out, d0, d1, init, op0, op1):
        run("v", lambda: g.vector.tensor_tensor_scan(out=ap(out), data0=ap(d0), data1=ap(d1), initial=val(init), op0=op0, op1=op1), rd(d0, d1, init), [out])

    def act(out, a, func=X, bias=0.0, scale=1.0, acc=None):
        if len(out) == 2:
            w, m = wr(out)
            run("s", lambda: g.scalar.activation(out=ap(out), in_=ap(a), func=func), rd(a) + m, w)
        elif acc is None:
            run("s", lambda: g.scalar.activation(out=ap(out), in_=ap(a), func=func, bias=val(bias), scale=val(scale)), rd(a, bias, scale), [out])
        else:
            run("s", lambda: g.scalar.activation(out=ap(out), in_=ap(a), func=func, bias=val(bias), scale=val(scale), accum_out=ap(acc)), rd(a, bias, scale), [out, acc])

    def mm(out, lhsT, rhs, start, stop):
        run("t", lambda: g.tensor.matmul(out=ap(out), lhsT=ap(lhsT), rhs=ap(rhs), start=start, stop=stop), rd(lhsT, rhs), [out])

    def chain(out, pairs, start=True, stop=True):
        for n, (l, r) in enumerate(pairs):
            mm(out, l, r, start and n == 0, stop and n == len(pairs) - 1)

    def iota(o, pattern, base, cm):
        if SCRATCH[o[0]][2] != i32:
            run("g", lambda: g.iota(ap(o), pattern, base, cm, allow_small_or_imprecise_dtypes=True), [], [o])
        else:
            run("g", lambda: g.iota(ap(o), pattern, base, cm), [], [o])

    def Z(buf, i):
        return R(buf, 16 - i, 144 - i)

    def tolist(out, x, n):
        chain(out, [(Z("Zs", i), R(x, i, n, 16)) for i in range(16)])

    dma("y", T.FI[:, :], T.fr[:, :], [], [R("FI")])
    dma("y", T.CLI[:, :], T.cl[:, :], [], [R("CLI")])
    dma("y", T.S[:, 0:3072], T.xv[:, :], [], [R("S", 0, 3072)])
    dma("y", T.thi[:, :], T.th[:, :], [], [R("thi")])

    iota(R("pci"), [[0, 1]], 0, 1)
    iota(R("row"), [[1, 144]], -16, 0)
    iota(R("grow"), [[1, 8], [0, 16]], 0, 0)
    iota(R("mrow"), [[0, 8], [1, 16]], 0, 0)
    iota(R("r16"), [[1, 16]], 0, 0)
    iota(R("q8"), [[1, 256]], int(BIG), 0)
    iota(R("W", 0, 256), [[0, 256]], 0, 0)
    iota(R("W", BZ, BZ + 192), [[0, 192]], 0, 0)
    for t in range(3):
        iota(R("SW%d" % t, 0, RW), [[0, RW]], 0, 0)
    iota(R("J129"), [[1, 128]], 129, 0)
    iota(R("kk"), [[0, 16], [1, 16]], 0, 0)
    iota(R("K15"), [[0, 16], [-1, 16]], 15, 0)
    iota(R("du"), [[16, 32]], 6144, 0)
    iota(R("VD"), [[0, 4608]], 8, 0)
    ts(R("pmi"), R("pci"), 15, O.bitwise_and)
    ts(R("pgi"), R("pci"), 4, O.arith_shift_right)
    cp(R("pc"), R("pci"))
    cp(R("pm"), R("pmi"))
    cp(R("pg"), R("pgi"))
    ts(R("p16"), R("pc"), 16.0, O.mult)
    ts(R("pg16"), R("pg"), 16.0, O.mult)
    ts(R("Blk"), R("grow"), col("pg", 0), O.is_equal)
    ts(R("Eye"), R("row", 16, 144), col("pc", 0), O.is_equal)
    ts(R("Z8"), R("row", P=8), R("p16", P=8), O.is_equal)
    ts(R("RM"), R("r16"), col("pm", 0), O.is_equal)
    ts(R("LM"), R("r16"), col("pm", 0), O.is_gt)
    ts(R("t1"), R("mrow"), col("pm", 0), O.is_le, -1.0, O.mult)
    ts(R("t2"), R("Eye"), -BIG - 1.0, O.mult)
    cp(R("FB"), R("FI"))
    chain(R("p0", 0, 96), [(R("Z8", 16 - i, 144 - i), R("FB", i, 1536, 16)) for i in range(16)])
    ts(R("t3"), R("Eye"), -1.0, O.mult, 1.0, O.add)
    tt(R("t4"), R("t1"), R("Blk"), O.mult)
    fill(R("one"), 1.0)
    tt(R("t5"), R("t4"), R("t3"), O.mult)
    ts(R("NI"), R("Eye"), -32.0, O.mult)
    tt(R("NTB"), R("t5"), R("t2"), O.add)
    ts(R("Zw"), R("row"), col("pg16", 0), O.is_equal)
    ts(R("k15"), R("pm"), -1.0, O.mult, 15.0, O.add)
    cp(R("F"), R("p0", 0, 96))
    act(R("S", 3072, 4608), R("S", 0, 1536), AF.Identity, 63.0, -1.0)
    for i in range(16):
        act(R("BC", 128 * i, 128 * i + 128), R("Blk"), X, 0.0, col("RM", i))
    for i in range(1, 16):
        act(R("LT", 128 * i, 128 * i + 128), R("Blk"), X, 0.0, col("LM", i))

    def consts():
        ts(R("Zs"), R("Zw"), 0.0625, O.mult)
        ts(R("Zn"), R("Zw"), -1.0, O.mult)
        cp(R("Tc"), R("thi"))
        ts(R("Z16"), R("Zw"), 16.0, O.mult)
        ts(R("Tb"), R("Tc"), -1.0, O.mult, 1.0, O.add)

    def late_consts():
        ts(R("S", 4608, 6144), R("S", 1536, 3072), -1.0, O.mult, 63.0, O.add)
        ts(R("RST"), R("kk"), 0.5, O.is_gt)
        ts(R("dum"), R("du"), col("pm", 0), O.add)
        fill(R("o16"), 0.0625)
        ts(R("E64"), R("Eye"), 64.0, O.mult)

    def flags():
        ts(R("FL", 0, 96), R("F"), 0.0, O.is_equal)
        ts(R("FL", 192, 288), R("F"), 4.0, O.is_ge)
        ts(R("g1"), R("F"), 1.0, O.is_ge)
        tt(R("FL", 96, 192), R("g1"), R("FL", 192, 288), O.subtract)

    def counts():
        mm(R("p1", 0, 288), R("Blk"), R("FL"), True, True)
        mm(R("p0", 0, 288), R("NTB"), R("FL"), True, True)

    def codes(t):
        u = {0: 16 * t, 1: 32 * t, 2: 0}
        for c, base in ((0, BA), (1, BZ), (2, BD)):
            o = 96 * c
            scan(R("IL", o + u[c], o + 96), R("one", u[c], 96), R("p1", o + u[c], o + 96), BIG + base, O.mult, O.add)
        for c in (0, 1):
            o = 96 * c
            if u[c]:
                scan(R("IL", o, o + u[c]), R("one", 0, u[c]), R("p1", o, o + u[c]), col("IL", o + 95), O.mult, O.add)
        tt(R("rz"), R("IL"), R("p0", 0, 288), O.add)
        tt(R("m1"), R("rz", 0, 96), R("rz", 96, 192), O.min)
        tt(R("code"), R("m1"), R("rz", 192, 288), O.min)
        cp(R("cU"), R("code"))

    def pack(t):
        ts(R("inv"), R("q8"), col("IL", (16 * t or 96) - 1), O.is_ge)
        if t == 0:
            cp((R("W", 0, 4608), R("cU")), R("CLI"))
        else:
            act((R("W", 0, 4608), R("cU")), R("CLF"), AF.Silu)

    flags()
    counts()
    consts()
    codes(0)
    late_consts()
    pack(0)

    for t in range(3):
        more = t < 2
        base = BR + RW * t
        add = 64.0 if t else 0.0
        sw = "SW%d" % t
        TAB = R("S", 0, 6144)

        def indicate(a0, a1):
            ts(R("ind", 16 * a0, 16 * a1), R("s", 16 * a0, 16 * a1), col("Tc", 0), O.is_ge)
            chain(R("p2", a0, a1), [(R("Eye"), R("ind", 16 * a0 + k, 16 * a1, 16)) for k in range(16)])

        def tots(a0, a1):
            chain(R("p4", a0 // 2, a1 // 2), [(Z(z, k), R("s", 16 * a0 + o + k, 16 * a1, 32)) for z, o in (("Zw", 16), ("Zn", 0)) for k in range(16)])

        def planes(k0, k1):
            for k in range(k0, k1):
                tt(R("pr", k, 16 * SPL, 16), R("s", k, 16 * SPL, 16), R("p2", 256, 256 + SPL), O.mult)

        def relus():
            w, n = 256 - SPL, 0
            for k in range(16):
                o = R(("p0", "p1", "p7", "p5")[k % 4], n, n + w)
                n += w if k % 4 == 3 else 0
                n = 0 if n + w > 512 else n
                chain(o, [(R("Eye"), R("s", 16 * SPL + k, 4096, 16)), (R("E64"), R("failB", SPL, 256))])
                act(R("pr", 16 * SPL + k, 4096, 16), o, AF.Relu, -64.0)

        def sums(a0, a1, stop):
            chain(R("p6", 0, 256), [(Z("Z16", i), R("pr", 256 * i, 256 * i + 256)) for i in range(a0 // 16, a1 // 16)], False, stop)

        def frozen(z0, z1):
            act(R("indz", 16 * z0, 16 * z1), (TAB, R("offZ", z0, z1)), AF.Relu, col("Tb", 0))

        def frozen_sums(z0, z1):
            chain(R("p5", z0, z1), [(R("Eye"), R("indz", 16 * z0 + k, 16 * z1, 16)) for k in range(16)])

        ts(R("offA"), R("W", 0, 256), MAGIC, O.add, -MAGIC - add, O.add)
        cp(R("s", 0, 16 * A1), (TAB, R("offA", 0, A1)))
        for a0, a1 in ((A1, A2), (A2, 256)):
            act(R("s", 16 * a0, 16 * a1), (TAB, R("offA", a0, a1)))
        ts(R("offZ"), R("W", BZ, BZ + 192), MAGIC, O.add, -MAGIC - add, O.add)
        frozen(0, ZC)
        indicate(0, A1)
        tots(0, 128)
        ts(R("whi"), R("W", 0, 256), -add, O.add)
        tt(R("diff"), R("W", 1, 256, 2), R("W", 0, 256, 2), O.subtract)
        indicate(A1, A2)
        tt(R("wlo"), R("W", 0, 256), R("whi"), O.subtract)
        indicate(A2, 256)
        ts(R("failB"), R("p2", 0, 256), 0.5, O.is_lt)
        chain(R("p3", 0, 256), [(R("NI"), R("inv")), (R("Blk"), R("failB"))])
        tots(128, 256)
        ts(R("p2", 256, 512), R("p2", 0, 256), 0.5, O.is_lt)
        relus()
        planes(0, 4)
        ts(R("QB", 256, 512), R("p3", 0, 256), 5.5, O.is_gt)
        tt(R("vb"), R("QB", 256, 512, 2), R("QB", 257, 512, 2), O.mult)
        planes(4, 5)
        scan(R("QB", 0, 128), R("one"), R("vb"), 0.0, O.mult, O.add)
        ts(R("nvb"), R("vb"), 0.5, O.is_lt)
        planes(5, 6)
        tt(R("QB", 128, 256), R("nvb"), R("J129"), O.mult)
        tolist(R("p3", 256, 288), "QB", 512)
        planes(6, 10)
        ts(R("p4", 128, 256), R("p4", 0, 128), 0.0, O.is_gt)
        planes(10, 11)
        tt(R("mj"), R("diff"), R("p4", 128, 256), O.mult)
        cp(R("jx"), R("p3", 256, 264))
        planes(11, 12)
        tt(R("jy"), R("jx"), R("p3", 264, 272), O.add)
        cp(R(sw, 0, 1), R("QB", 127, 128))
        planes(12, 13)
        cp(R("jc"), R("jy"))
        planes(13, 14)
        tt((R(sw), R("jc")), R("mj"), R("W", 0, 256, 2), O.add)
        dst = T.cores[(rank + 1 + t) % N]
        src = T.cores[(rank - 1 - t) % N]
        need("g", [R(sw, 0, RW)], [], "x")
        rid, pid, _ = topo.addr(dst)
        g.remote_dma(T.W[:, base:base + RW], T[sw][:, 0:RW], T.sem["arr%d" % t], T.sem.snd, pid, rid, sum(1 << e for e in topo.engines(core, dst)[::2]))
        note("rem", ("arr%d" % t, len(topo.engines(src, core)[::2])), [], [R("W", base, base + RW)])
        frozen(ZC, 192)
        act(R("VD", 0, 256), R("QB", 256, 512), AF.Identity, 9.0, -1.0)
        planes(14, 16)
        frozen_sums(0, ZC)
        mm(R("p6", 0, 256), R("Eye"), R("K15"), True, False)
        sums(SPL, 256, False)
        frozen_sums(ZC, 192)
        sums(0, 48, False)
        ts(R("failz"), R("p5", 0, 192), 0.5, O.is_lt)
        mm(R("p5", 256, 448), R("Blk"), R("failz"), True, True)
        sums(48, SPL, True)
        ts(R("VD", BZ, BZ + 192), R("p5", 256, 448), 5.5, O.is_le, 9.0, O.mult)
        act(R("DR"), (R("VD"), R("cU")))
        act(R("nviol"), R("QB", 256, 512), AF.Identity, 1.0, -1.0, R("cnt"))
        act(R("fail8"), R("failB"), X, 0.0, 8.0)
        scan(R("km"), R("RST"), R("p6", 0, 256), 0.0, O.mult, O.max)
        cp(R("ki"), R("km", 15, 256, 16))
        ts(R("ka"), R("ki"), 15, O.bitwise_and)
        cp(R("kb"), R("ka"))
        for i in range(16):
            mm(R("p6", 16 * i, 16 * i + 16), R("BC", 128 * i, 128 * i + 128), R("kb"), True, True)
        ts(R("p6", 256, 512), R("p6", 0, 256), col("k15", 0), O.is_equal)
        tt(R("HL", 0, 256), R("whi"), R("p6", 256, 512), O.mult)
        tt(R("HL", 256, 512), R("wlo"), R("p6", 256, 512), O.mult)
        ts(R("thr"), R("W", base, base + 1), float(BD), O.add)
        ts(R("tk"), R("rz", 192, 288), col("thr", 0), O.is_lt, float(base + 1 - BD), O.mult)
        tt(R("code2"), R("code"), R("tk"), O.add)
        cp(R("cU2"), R("code2"))
        act(R("CLF"), (R("W", 0, base + RW), R("cU2")), AF.Identity, (64.0, 0.0, MAGIC - 64.0)[t])
        tolist(R("p5", 0, 96), "DR", 1536)
        tt(R("f1"), R("F"), R("p5", 0, 96), O.add)
        tt(R("f2"), R("f1"), R("tk"), O.subtract)
        ts(R("F"), R("f2"), -8.0, O.add, 0.0, O.max)
        chain(R("p7", 0, 256), [(R("Blk"), R("HL", 0, 256)), (R("Blk"), R("HL", 256, 512))])
        chain(R("p2", 0, 32), [(Z("Zw", i), R("HL", i, 512, 16)) for i in range(16)])
        if more:
            flags()
            counts()
        ts(R("nr"), R("p7", 0, 256), 3071.5 + add, O.is_ge, -3072.0, O.mult)
        ts(R("litH"), R("p2", 0, 16), MAGIC, O.add, -MAGIC - add, O.add)
        tt(R("vr"), R("nr"), R("p7", 0, 256), O.add)
        tt(R("litL"), R("litH"), R("p2", 16, 32), O.add)
        if more:
            codes(t + 1)
            pack(t + 1)
        ts(R("vU"), R("vr"), MAGIC, O.add, -MAGIC, O.add)
        ts(R("ng"), R("litL"), 3072.0, O.is_ge, -3072.0, O.mult)
        cp(R("litU"), R("litL"))
        tt(R("vL"), R("litL"), R("ng"), O.add)
        ts(R("vM"), R("vL"), 1.0 + add, O.add)
        tt(R("vN"), R("vM"), R("p3", 272, 288), O.mult)
        ts(R("vQ"), R("vN"), -1.0, O.add)
        for c in range(16):
            ts(R("E", 272 * c, 256 * c + 256), R("vU", 16 * c, 256), col("vQ", c), O.is_equal)
        mm(R("p4", 0, 256), R("Eye"), R("nviol"), True, False)
        for c in range(15):
            mm(R("p4", 16 * c + 16, 256), R("Blk"), R("E", 272 * c + 16, 256 * c + 256), False, False)
        tt(R("us"), (TAB, R("litU")), R("fail8"), O.add)
        tt(R("cm"), R("vL"), R("ng"), O.add)
        ts(R("UP", 0, 256), R("us"), 63.0, O.min)
        ts(R("cN"), R("cm"), 3072.0, O.add)
        ts(R("UP", 256, 512), R("UP", 0, 256), -1.0, O.mult, 63.0, O.add)
        for i in range(1, 16):
            mm(R("p4", i, 256, 16), R("LT", 128 * i, 128 * i + 128), R("E", i, 4096, 272), False, False)
        mm(R("p4", 0, 256), R("Eye"), R("nviol"), False, True)
        tt(R("y", 0, 16), R("litL"), R("dum", 0, 16), O.subtract)
        tt(R("y", 16, 32), R("cN"), R("dum", 16, 32), O.subtract)
        if more:
            mm(R("p3", 300, 301), R("o16"), R("cnt"), True, True)
        ts(R("mv"), R("p4", 0, 256), 0.5, O.is_lt)
        tolist(R("p7", 256, 272), "mv", 256)
        if more:
            ts(R("ai"), R("p3", 300, 301), -1.0, O.mult, 2048.0, O.add)
        tt(R("o1", 0, 16), R("y", 0, 16), R("p7", 256, 272), O.mult)
        tt(R("o1", 16, 32), R("y", 16, 32), R("p7", 256, 272), O.mult)
        if more:
            ts(R("a3"), R("ai"), 3, O.bitwise_and)
        tt(R("o2"), R("o1"), R("dum"), O.add)
        if more:
            tt(R("Tc"), R("a3"), R("thi"), O.add)
        cp(R("oU"), R("o2"))
        if more:
            ts(R("Tb"), R("Tc"), -1.0, O.mult, 1.0, O.add)
        cp((R("S"), R("oU")), R("UP"))

    act(R("CLF"), R("CLF"), AF.Identity, -MAGIC)
    dma("y", T.yc[:, :], T.CLF[:, :], [R("CLF")], [])
    for c in range(3):
        for i in range(16):
            mm(R("p%d" % c, i, 512, 16, 8), R("BC", 128 * i, 128 * i + 128, 16), R("F", 32 * c, 32 * c + 32), True, True)
        act(R("YF", 512 * c, 512 * c + 512), R("p%d" % c, 0, 512, 1, 8))
    dma("y", T.yf[:, :], T.YF[:, :], [R("YF")], [])
    dma("y", T.yx[:, :], T.S[:, 0:3072], [R("S", 0, 3072)], [])
    sent = sum(len(topo.engines(core, T.cores[(rank + 1 + t) % N])[::2]) for t in range(3))
    finish([("snd", sent)] + [("arr%d" % t, len(topo.engines(T.cores[(rank - 1 - t) % N], core)[::2])) for t in range(3)])
